import numpy as np, ml_dtypes
CORES = [122,123,126,250,251,254,378,379,382,506,507,510]
N = 12
K, F = 2, 64
def setup_inputs(rng):
    return {"gr": rng.standard_normal((N, K, 128, N * F), dtype=np.float32).astype(ml_dtypes.bfloat16)}
def setup_inputs_big(rng):
    d = setup_inputs(rng)
    for k in ("gr",): d[k] = (d[k].astype(np.float32) * 1048576.0).astype(d[k].dtype)
    return d
def setup_inputs_small(rng):
    d = setup_inputs(rng)
    for k in ("gr",): d[k] = (d[k].astype(np.float32) * (1 / 1048576.0)).astype(d[k].dtype)
    return d
def reference(gr):
    s = gr.astype(np.float64).sum(axis=(0, 1))
    return {"y": np.stack([s[:, F * r:F * r + F] for r in range(N)]).astype(np.float32 if gr.dtype != np.float64 else np.float64)}

from concourse.bass import DstId, RemoteDMATransfer
from concourse.mybir import AluOpType

F = 64
NL = 3
NH = 4
P = 128

SCRATCH = {
    "G":   ("sbuf", [P, 2, NH, NL, F], "bfloat16"),
    "S":   ("sbuf", [P, NL, NH, F], "float32"),
    "L1a": ("sbuf", [P, NL - 1, F], "float32"),
    "L1b": ("sbuf", [P, NL - 1, NH - 1, F], "float32"),
    "L2a": ("sbuf", [P, F], "float32"),
    "L2b": ("sbuf", [P, F], "float32"),
    "L3":  ("sbuf", [P, F], "float32"),
    "P1":  ("sbuf", [P, F], "float32"),
    "P2":  ("sbuf", [P, F], "float32"),
    "P3":  ("sbuf", [P, F], "float32"),
    "Y":   ("sbuf", [P, F], "float32"),
}
SEMAPHORES = ["ldA", "ldB", "kA", "kA0", "kB", "kB0", "a1a", "a1b", "a2a", "a2b", "a3", "sent",
              "p1", "p2", "p3", "yv", "st"]

DIAG, SW, CB, OWN = 0, 1, 2, 3


def _bits(mask):
    return [e for e in range(mask.bit_length()) if (mask >> e) & 1]


def _mask(engines):
    m = 0
    for e in engines:
        m |= 1 << e
    return m


def rank_program(g, core, T, topo):
    if T.rank_of(core) is None:
        return
    cores = list(T.cores)
    sem = T.sem
    add = AluOpType.add

    def place(c):
        return (topo.host(c), topo.chip(c))

    def mates_of(c):
        return [d for d in cores if place(d) == place(c)]

    def block(c):
        return T.rank_of(mates_of(c)[0]) // NL

    chipmates = mates_of(core)
    j = chipmates.index(core)
    others = [x for x in range(NL) if x != j]
    twins = [c for c in cores if c != core and mates_of(c).index(c) == j]
    t_sw = [c for c in twins if topo.same_plane(core, c)][0]
    t_dg = [c for c in twins if not topo.may_write(core, c)][0]
    t_cb = [c for c in twins if c != t_sw and c != t_dg][0]
    hb = {DIAG: block(t_dg), SW: block(t_sw), CB: block(t_cb), OWN: block(core)}

    on_my_die = [c for c in chipmates if topo.die(c) == topo.die(core)]
    if on_my_die.index(core) % 2 == 0:
        first, s_first, second, s_second = t_sw, SW, t_cb, CB
    else:
        first, s_first, second, s_second = t_cb, CB, t_sw, SW

    off = _bits(topo.mask(core, first) & topo.mask(core, second))
    rest = [e for e in _bits(topo.mask(core, chipmates[others[0]])) if e not in off]

    def dst_id(d):
        rid, pid = topo.addr(d, core)
        return DstId(rid=rid, pnc=pid)

    W = NL * F
    later = sorted(hb[s] for s in (SW, CB, OWN))
    runs = []
    for b in later:
        if runs and runs[-1][1] == b:
            runs[-1][1] = b + 1
        else:
            runs.append([b, b + 1])
    for k, q in ((0, g.sync), (1, g.scalar)):
        b = hb[DIAG]
        q.dma_start(T.G[:, k, b:b + 1], T.gr[k, :, W * b:W * (b + 1)]).then_inc(sem.ldA, 16)
        for lo, hi in runs:
            q.dma_start(T.G[:, k, lo:hi], T.gr[k, :, W * lo:W * hi]).then_inc(sem.ldB, 16)

    v = g.vector
    psel = slice(others[0], others[1] + 1, others[1] - others[0])

    def ksum(who, s, done):
        v.tensor_tensor(T.S[:, who, s, :], T.G[:, 0, hb[s], who, :], T.G[:, 1, hb[s], who, :], add).then_inc(done, 1)

    v.wait_ge(sem.ldA, 32)
    ksum(psel, DIAG, sem.kA)
    ksum(j, DIAG, sem.kA0)
    v.wait_ge(sem.ldB, 32 * len(runs))
    for s in (SW, CB, OWN):
        ksum(psel, s, sem.kB)
    for s in (s_first, s_second, OWN):
        ksum(j, s, sem.kB0)

    sent = 0

    def to_mates(engines, src_of, dst_of, arrived):
        n = 0
        trs = []
        for i, x in enumerate(others):
            es = engines[i::len(others)]
            slot = [y for y in range(NL) if y != x].index(j)
            trs.append(RemoteDMATransfer(dst_ids=[dst_id(chipmates[x])], dma_engine_mask=_mask(es),
                                         remote_sem=arrived, src=src_of(x), dst=dst_of(slot)))
            n += len(es)
        g.remote_dma_fused(trs, local_sem=sem.sent)
        return n

    def fold_to(d, srcs, dst, arrived):
        g.remote_dma_fused([RemoteDMATransfer(dst_ids=[dst_id(d)], dma_engine_mask=_mask(off), remote_sem=arrived,
                                              srcs=srcs, dsts=[dst], alu_op=1)], local_sem=sem.sent)
        return len(off)

    def chip_sum(s):
        if s == DIAG:
            return [T.S[:, j, s, :]] + [T.L1a[:, i, :] for i in range(NL - 1)]
        return [T.S[:, j, s, :]] + [T.L1b[:, i, s - 1, :] for i in range(NL - 1)]

    n1a = len(off[0::2]) + len(off[1::2])
    n1b = len(rest[0::2]) + len(rest[1::2])

    g.wait_ge(sem.kA, 1)
    sent += to_mates(off, lambda x: T.S[:, x, DIAG, :], lambda i: T.L1a[:, i, :], sem.a1a)
    g.wait_ge(sem.kB, 3)
    sent += to_mates(rest, lambda x: T.S[:, x, SW:OWN + 1, :], lambda i: T.L1b[:, i, :, :], sem.a1b)
    g.wait_ge(sem.kA0, 1)
    g.wait_ge(sem.a1a, n1a)
    sent += fold_to(first, chip_sum(DIAG), T.L2a[:, :], sem.a2a)
    g.wait_ge(sem.kB0, 3)
    g.wait_ge(sem.a1b, n1b)
    sent += fold_to(first, chip_sum(s_first), T.L2b[:, :], sem.a2b)
    g.wait_ge(sem.a2a, len(off))
    sent += fold_to(second, chip_sum(s_second) + [T.L2a[:, :]], T.L3[:, :], sem.a3)

    v.wait_ge(sem.kB0, 3)
    v.wait_ge(sem.a1b, n1b)
    v.tensor_tensor(T.P1[:, :], T.S[:, j, OWN, :], T.L1b[:, 0, OWN - 1, :], add).then_inc(sem.p1, 1)
    v.wait_ge(sem.p1, 1)
    v.tensor_tensor(T.P2[:, :], T.P1[:, :], T.L1b[:, 1, OWN - 1, :], add).then_inc(sem.p2, 1)
    v.wait_ge(sem.p2, 1)
    v.wait_ge(sem.a2b, len(off))
    v.tensor_tensor(T.P3[:, :], T.P2[:, :], T.L2b[:, :], add).then_inc(sem.p3, 1)
    v.wait_ge(sem.p3, 1)
    v.wait_ge(sem.a3, len(off))
    v.tensor_tensor(T.Y[:, :], T.P3[:, :], T.L3[:, :], add).then_inc(sem.yv, 1)

    g.sync.wait_ge(sem.yv, 1)
    g.sync.dma_start(T.y[:, :], T.Y[:, :]).then_inc(sem.st, 16)
    g.sync.wait_ge(sem.st, 16)
    g.wait_ge(sem.sent, sent)
